import numpy as np
import ml_dtypes


def mxq(x, axis, fmt="e4m3"):
    dtype, down = {"e4m3": (ml_dtypes.float8_e4m3fn, 7), "e5m2": (ml_dtypes.float8_e5m2, 14)}[fmt]
    v = np.moveaxis(np.asarray(x, np.float32).astype(ml_dtypes.bfloat16).astype(np.float64), axis, -1)
    blocks = v.reshape(v.shape[:-1] + (-1, 32))
    amax = np.abs(blocks).max(-1, keepdims=True)
    byte = np.maximum(np.where(amax > 0, np.frexp(amax)[1] - 1 + 127, 0) - down, 1)
    scale = np.exp2(byte - 127.0)
    codes = (blocks / scale).astype(np.float32).astype(dtype).astype(np.float64)
    return np.moveaxis((codes * scale).reshape(v.shape), -1, axis)


WIDE = False


def mx_kscale(k):
    if not WIDE:
        return np.ones(k)
    levels = np.array([10, -10, 5, -5, 0])
    if k % 512:
        return np.exp2(np.random.permutation(np.resize(levels, k // 32))).repeat(32)
    a = np.empty((k // 512, 16))
    for p in range(k // 512):
        a[p, :8] = np.random.permutation(np.resize(levels, 8))
        for g in range(8):
            far = levels[np.abs(levels - a[p, g]) >= 10]
            a[p, g + 8] = far[np.random.randint(len(far))]
    return np.exp2(a.ravel()).repeat(32)


def f64(x):
    return np.asarray(x).astype(np.float64)


def striped(idx):
    return np.tile(idx.reshape(-1, 16).T, (8, 1)).astype(np.uint16)


def unstriped(offs):
    return offs[:16].T.reshape(-1).astype(np.int64)


def pack_weight(w):
    k, n = w.shape
    w = f64(np.asarray(w, np.float32).astype(ml_dtypes.bfloat16)).reshape(k // 32, 32, n)
    amax = np.abs(w).max(1)
    byte = np.clip(np.where(amax > 0, np.frexp(amax)[1] - 1 + 127 - 7, 1), 1, 254)
    scaled = (w * np.exp2(127.0 - byte)[:, None, :]).reshape(k, n).astype(np.float32)
    words = np.ascontiguousarray(scaled.reshape(k // 512, 128, 4, n).transpose(0, 1, 3, 2)).astype(ml_dtypes.float8_e4m3fn).view(np.uint8)
    return words, np.ascontiguousarray(byte.astype(np.uint8).reshape(k // 512, 16, n))


def unpack_weight(words, scales):
    g, p, n, _ = words.shape
    vals = np.ascontiguousarray(words).view(ml_dtypes.float8_e4m3fn).astype(np.float64) * np.repeat(np.exp2(scales.astype(np.float64) - 127.0), 8, axis=1)[..., None]
    return vals.transpose(0, 1, 3, 2).reshape(g * 512, n)


K, T, E, C, N = 3072, 768, 6, 128, 128


def by_expert(wq, xq):
    return np.concatenate([wq[e].T @ xq[:, e * C:(e + 1) * C] for e in range(E)], axis=1)


def setup_inputs():
    n = np.random.standard_normal
    s = mx_kscale(K)[:, None]
    packed = [pack_weight(m) for m in n((E, K, N)) / np.sqrt(K) / s[None]]
    return {
        "xT": (n((K, T)) * s).astype(np.float32),
        "w_words": np.stack([m[0] for m in packed]),
        "w_scales": np.stack([m[1] for m in packed]),
        "gate": np.tile(np.random.uniform(0.2, 1.0, E * C), (N, 1)).astype(np.float32),
        "offs": striped(np.random.permutation(T)[:E * C]),
    }


def reference(xT, w_words, w_scales, gate, offs):
    idx = unstriped(offs)
    xq = mxq(f64(xT)[:, idx], 0, "e4m3")
    w = np.stack([unpack_weight(w_words[e], w_scales[e]) for e in range(E)])
    y = by_expert(w, xq)
    out = np.zeros((N, T))
    out[:, idx] = f64(gate) * y
    return out

@@ -1,0 +1,117 @@
+from contextlib import ExitStack
+
+import concourse.mybir as mybir
+
+K, T, E, C, N = 3072, 768, 6, 128, 128
+FLOPS = 2 * K * N * E * C
+
+F32 = mybir.dt.float32
+BF16 = mybir.dt.bfloat16
+I32 = mybir.dt.int32
+U32 = mybir.dt.uint32
+U16 = mybir.dt.uint16
+U8 = mybir.dt.uint8
+FP8X4 = mybir.dt.float8_e4m3fn_x4
+MULT = mybir.AluOpType.mult
+
+P = 128
+R = 4
+A = K // (P * R)
+HALF = E * C // 2
+EH = E // 2
+V_TOK = (256, 128, 128, 128, 128, 256)
+
+
+def tile_routed_moe_kernel(tc, xT, w_words, w_scales, gate, offs, out):
+    nc = tc.nc
+    with ExitStack() as ctx:
+        keep = ctx.enter_context(tc.tile_pool(name="keep", bufs=1))
+        psum = ctx.enter_context(tc.psum_pool(name="psum", bufs=1))
+
+        offsets = keep.tile([P, E * C // 16], U16, name="offsets")
+        w = keep.tile([P, E, A, N], I32, name="w", align_bytes=256)
+        ws = keep.tile([P, E * A, N // 4], I32, name="ws", align_bytes=256)
+        gt = keep.tile([P, E * C], F32, name="gt")
+        xs = [keep.tile([P, T], U8, name=f"xs{g}", align_bytes=256) for g in range(2)]
+        gs = [keep.tile([P, E * C], U8, name=f"gs{g}", align_bytes=256) for g in range(2)]
+        raw = [keep.tile([P, R, T], F32, name=f"raw{a}", align_bytes=256) for a in range(A)]
+        grp = [keep.tile([P, T, R], BF16, name=f"grp{a}", align_bytes=256) for a in range(A)]
+        xw = [keep.tile([P, T], U32, name=f"xw{a}", align_bytes=256) for a in range(A)]
+        gw = [keep.tile([P, E * C], U32, name=f"gw{a}", align_bytes=256) for a in range(A)]
+        z = keep.tile([P, E * C], F32, name="z")
+        window = keep.tile([P, T], F32, name="window")
+        acc = [psum.tile([P, HALF], F32, name=f"acc{h}") for h in range(2)]
+
+        nc.vector.memset(ws[:], 0)
+        for g in range(2):
+            nc.gpsimd.memset(xs[g][:], 0)
+
+        xv = xT.rearrange("(a p t) n -> a p t n", p=P, t=R)
+        for a in range(A):
+            cuts = (0, 512, T) if a in (0, A - 1) else (0, T)
+            for lo, hi in zip(cuts[:-1], cuts[1:]):
+                nc.sync.dma_start(out=raw[a][:, :, lo:hi], in_=xv[a][:, :, lo:hi])
+            if a == 0:
+                nc.sync.dma_start(offsets[:], offs)
+        sv = w_scales.bitcast(I32).rearrange("e a q n -> q (e a) n")
+        for q in range(4):
+            nc.sync.dma_start(out=ws[32 * q : 32 * q + 4], in_=sv[4 * q : 4 * q + 4])
+        for e in range(E):
+            if e == EH:
+                nc.sync.dma_start(out=gt[:], in_=gate)
+            nc.sync.dma_start(out=w[:, e], in_=w_words[e].rearrange("a p n r -> p a (n r)").bitcast(I32))
+
+        def cast(engine_copy, a, lo, hi):
+            engine_copy(
+                out=grp[a][:, lo:hi, :].rearrange("p (c i) t -> p c t i", i=4),
+                in_=raw[a][:, :, lo:hi].rearrange("p t (c i) -> p c t i", i=4),
+            )
+
+        def quantize(a, lo, hi):
+            nc.vector.quantize_mx(
+                out=xw[a][:, lo:hi].bitcast(FP8X4),
+                scales=xs[a // 4][4 * (a % 4) : P, lo:hi],
+                in_=grp[a][:, lo:hi, :].rearrange("p n t -> p (n t)"),
+            )
+
+        def gather(dst, src, h):
+            nc.vector.tensor_copy(dst[:, h * HALF : (h + 1) * HALF], src[:].indirect(offsets[:, h * HALF // 16 : (h + 1) * HALF // 16]))
+
+        def multiply(h):
+            for e in range(h * EH, (h + 1) * EH):
+                slots = slice(e * C, (e + 1) * C)
+                for a in range(A):
+                    k = 4 * (a % 4)
+                    nc.tensor.matmul_mx(
+                        out=acc[h][:, (e - h * EH) * C : (e - h * EH + 1) * C],
+                        lhsT=w[:, e, a, :].bitcast(FP8X4),
+                        lhsT_scale=ws[:, e * A + a, :].bitcast(U8),
+                        rhs=gw[a][:, slots].bitcast(FP8X4),
+                        rhs_scale=gs[a // 4][k:P, slots],
+                        start=(a == 0),
+                        stop=(a == A - 1),
+                    )
+
+        for a in range(A):
+            split = T - V_TOK[a]
+            for lo, hi in ((0, 512), (512, T)):
+                if split > lo:
+                    cast(nc.scalar.copy, a, lo, min(hi, split))
+            cast(nc.vector.tensor_copy, a, split, T)
+            quantize(a, 0, 512)
+            quantize(a, 512, T)
+            if a < A - 1:
+                for h in range(2):
+                    gather(gw[a], xw[a], h)
+            if a == 3:
+                for h in range(2):
+                    gather(gs[0], xs[0], h)
+        for h in range(2):
+            gather(gs[1], xs[1], h)
+            gather(gw[A - 1], xw[A - 1], h)
+            multiply(h)
+        for h in range(2):
+            half = slice(h * HALF, (h + 1) * HALF)
+            nc.vector.tensor_tensor(z[:, half], acc[h][:], gt[:, half], MULT)
+            nc.vector.tensor_copy(window[:].indirect(offsets[:, h * HALF // 16 : (h + 1) * HALF // 16]), z[:, half])
+        nc.sync.dma_start(out=out, in_=window[:])

@@ -17,9 +17,26 @@ MULT = mybir.AluOpType.mult
 P = 128
 R = 4
 A = K // (P * R)
-HALF = E * C // 2
-EH = E // 2
-V_TOK = (256, 128, 128, 128, 128, 256)
+WIN = 1024
+GROUP = (0, 0, 1, 1, 1, 1)
+PLANE = (0, 4, 0, 4, 8, 12)
+LOADS = (
+    ((0, 256), (256, 512), (512, 768)),
+    ((0, 512), (512, 768)),
+    ((0, 768),),
+    ((0, 768),),
+    ((0, 768),),
+    ((0, 512), (512, 768)),
+)
+SHARE = (
+    ((0, 256, 512), (512, 640, 768)),
+    ((0, 288, 512), (512, 640, 768)),
+    ((0, 512, 512), (512, 576, 768)),
+    ((0, 512, 512), (512, 640, 768)),
+    ((0, 512, 512), (512, 640, 768)),
+    ((0, 320, 512), (512, 640, 768)),
+)
+BACK = ((0, 384), (384, 768))
 
 
 def tile_routed_moe_kernel(tc, xT, w_words, w_scales, gate, offs, out):
@@ -32,86 +49,93 @@ def tile_routed_moe_kernel(tc, xT, w_words, w_scales, gate, offs, out):
         w = keep.tile([P, E, A, N], I32, name="w", align_bytes=256)
         ws = keep.tile([P, E * A, N // 4], I32, name="ws", align_bytes=256)
         gt = keep.tile([P, E * C], F32, name="gt")
-        xs = [keep.tile([P, T], U8, name=f"xs{g}", align_bytes=256) for g in range(2)]
+        xs = [keep.tile([P, WIN], U8, name=f"xs{g}", align_bytes=256) for g in range(2)]
         gs = [keep.tile([P, E * C], U8, name=f"gs{g}", align_bytes=256) for g in range(2)]
         raw = [keep.tile([P, R, T], F32, name=f"raw{a}", align_bytes=256) for a in range(A)]
         grp = [keep.tile([P, T, R], BF16, name=f"grp{a}", align_bytes=256) for a in range(A)]
-        xw = [keep.tile([P, T], U32, name=f"xw{a}", align_bytes=256) for a in range(A)]
+        xw = [keep.tile([P, WIN], I32, name=f"xw{a}", align_bytes=256) for a in range(A)]
         gw = [keep.tile([P, E * C], U32, name=f"gw{a}", align_bytes=256) for a in range(A)]
-        z = keep.tile([P, E * C], F32, name="z")
+        z = [keep.tile([P, hi - lo], F32, name=f"z{lo}") for lo, hi in BACK]
         window = keep.tile([P, T], F32, name="window")
-        acc = [psum.tile([P, HALF], F32, name=f"acc{h}") for h in range(2)]
+        acc = [psum.tile([P, hi - lo], F32, name=f"acc{lo}") for lo, hi in BACK]
 
-        nc.vector.memset(ws[:], 0)
         for g in range(2):
             nc.gpsimd.memset(xs[g][:], 0)
+        for a in range(A):
+            nc.gpsimd.memset(xw[a][:, T:], 0)
+        nc.vector.memset(ws[:], 0)
 
         xv = xT.rearrange("(a p t) n -> a p t n", p=P, t=R)
-        for a in range(A):
-            cuts = (0, 512, T) if a in (0, A - 1) else (0, T)
-            for lo, hi in zip(cuts[:-1], cuts[1:]):
-                nc.sync.dma_start(out=raw[a][:, :, lo:hi], in_=xv[a][:, :, lo:hi])
-            if a == 0:
-                nc.sync.dma_start(offsets[:], offs)
         sv = w_scales.bitcast(I32).rearrange("e a q n -> q (e a) n")
-        for q in range(4):
-            nc.sync.dma_start(out=ws[32 * q : 32 * q + 4], in_=sv[4 * q : 4 * q + 4])
-        for e in range(E):
-            if e == EH:
-                nc.sync.dma_start(out=gt[:], in_=gate)
+
+        def load_x(a):
+            for lo, hi in LOADS[a]:
+                nc.sync.dma_start(out=raw[a][:, :, lo:hi], in_=xv[a][:, :, lo:hi])
+
+        def load_w(e):
             nc.sync.dma_start(out=w[:, e], in_=w_words[e].rearrange("a p n r -> p a (n r)").bitcast(I32))
 
+        def load_scales():
+            for q in range(4):
+                nc.sync.dma_start(out=ws[32 * q : 32 * q + 4], in_=sv[4 * q : 4 * q + 4])
+
+        load_x(0)
+        nc.sync.dma_start(offsets[:], offs)
+        for a in range(1, A):
+            load_x(a)
+        load_scales()
+        for e in range(E):
+            if e == E // 2:
+                nc.sync.dma_start(out=gt[:], in_=gate)
+            load_w(e)
+
         def cast(engine_copy, a, lo, hi):
-            engine_copy(
-                out=grp[a][:, lo:hi, :].rearrange("p (c i) t -> p c t i", i=4),
-                in_=raw[a][:, :, lo:hi].rearrange("p t (c i) -> p c t i", i=4),
-            )
+            if hi > lo:
+                engine_copy(
+                    out=grp[a][:, lo:hi, :].rearrange("p (c i) t -> p c t i", i=4),
+                    in_=raw[a][:, :, lo:hi].rearrange("p t (c i) -> p c t i", i=4),
+                )
 
         def quantize(a, lo, hi):
             nc.vector.quantize_mx(
                 out=xw[a][:, lo:hi].bitcast(FP8X4),
-                scales=xs[a // 4][4 * (a % 4) : P, lo:hi],
+                scales=xs[GROUP[a]][PLANE[a] : P, lo:hi],
                 in_=grp[a][:, lo:hi, :].rearrange("p n t -> p (n t)"),
             )
 
-        def gather(dst, src, h):
-            nc.vector.tensor_copy(dst[:, h * HALF : (h + 1) * HALF], src[:].indirect(offsets[:, h * HALF // 16 : (h + 1) * HALF // 16]))
+        def gather(dst, source, lo, hi):
+            nc.vector.tensor_copy(dst[:, lo:hi], source.indirect(offsets[:, lo // 16 : hi // 16]))
 
-        def multiply(h):
-            for e in range(h * EH, (h + 1) * EH):
+        def multiply(b):
+            first, last = BACK[b]
+            for e in range(first // C, last // C):
                 slots = slice(e * C, (e + 1) * C)
                 for a in range(A):
-                    k = 4 * (a % 4)
                     nc.tensor.matmul_mx(
-                        out=acc[h][:, (e - h * EH) * C : (e - h * EH + 1) * C],
+                        out=acc[b][:, e * C - first : (e + 1) * C - first],
                         lhsT=w[:, e, a, :].bitcast(FP8X4),
                         lhsT_scale=ws[:, e * A + a, :].bitcast(U8),
                         rhs=gw[a][:, slots].bitcast(FP8X4),
-                        rhs_scale=gs[a // 4][k:P, slots],
+                        rhs_scale=gs[GROUP[a]][PLANE[a] : P, slots],
                         start=(a == 0),
                         stop=(a == A - 1),
                     )
 
         for a in range(A):
-            split = T - V_TOK[a]
-            for lo, hi in ((0, 512), (512, T)):
-                if split > lo:
-                    cast(nc.scalar.copy, a, lo, min(hi, split))
-            cast(nc.vector.tensor_copy, a, split, T)
-            quantize(a, 0, 512)
-            quantize(a, 512, T)
+            for lo, mid, hi in SHARE[a]:
+                cast(nc.scalar.copy, a, lo, mid)
+                cast(nc.vector.tensor_copy, a, mid, hi)
+                quantize(a, lo, hi)
             if a < A - 1:
-                for h in range(2):
-                    gather(gw[a], xw[a], h)
-            if a == 3:
-                for h in range(2):
-                    gather(gs[0], xs[0], h)
-        for h in range(2):
-            gather(gs[1], xs[1], h)
-            gather(gw[A - 1], xw[A - 1], h)
-            multiply(h)
-        for h in range(2):
-            half = slice(h * HALF, (h + 1) * HALF)
-            nc.vector.tensor_tensor(z[:, half], acc[h][:], gt[:, half], MULT)
-            nc.vector.tensor_copy(window[:].indirect(offsets[:, h * HALF // 16 : (h + 1) * HALF // 16]), z[:, half])
+                gather(gw[a], xw[a][:].bitcast(U32), 0, E * C)
+            if a == 1:
+                gather(gs[0], xs[0][:], 0, E * C)
+        for lo, hi in ((0, 384), (384, 768)):
+            gather(gs[1], xs[1][:], lo, hi)
+            gather(gw[A - 1], xw[A - 1][:].bitcast(U32), lo, hi)
+        for b in range(len(BACK)):
+            multiply(b)
+        for b, (lo, hi) in enumerate(BACK):
+            nc.vector.tensor_tensor(z[b][:], acc[b][:], gt[:, lo:hi], MULT)
+            nc.vector.tensor_copy(window[:].indirect(offsets[:, lo // 16 : hi // 16]), z[b][:])
         nc.sync.dma_start(out=out, in_=window[:])

@@ -21,22 +21,22 @@ WIN = 1024
 GROUP = (0, 0, 1, 1, 1, 1)
 PLANE = (0, 4, 0, 4, 8, 12)
 LOADS = (
-    ((0, 256), (256, 512), (512, 768)),
+    ((0, 512), (512, 768)),
     ((0, 512), (512, 768)),
     ((0, 768),),
     ((0, 768),),
     ((0, 768),),
     ((0, 512), (512, 768)),
 )
-SHARE = (
-    ((0, 256, 512), (512, 640, 768)),
-    ((0, 288, 512), (512, 640, 768)),
-    ((0, 512, 512), (512, 576, 768)),
-    ((0, 512, 512), (512, 640, 768)),
-    ((0, 512, 512), (512, 640, 768)),
-    ((0, 320, 512), (512, 640, 768)),
+CASTS = (
+    (("S", 0, 192), ("V", 192, 512), ("S", 512, 640), ("V", 640, 768)),
+    (("S", 0, 288), ("V", 288, 512), ("S", 512, 640), ("V", 640, 768)),
+    (("S", 0, 512), ("S", 512, 576), ("V", 576, 768)),
+    (("S", 0, 512), ("S", 512, 640), ("V", 640, 768)),
+    (("S", 0, 512), ("S", 512, 640), ("V", 640, 768)),
+    (("S", 0, 320), ("V", 320, 512), ("S", 512, 640), ("V", 640, 768)),
 )
-BACK = ((0, 384), (384, 768))
+BACK = ((0, 384), (384, 640), (640, 768))
 
 
 def tile_routed_moe_kernel(tc, xT, w_words, w_scales, gate, offs, out):
@@ -62,7 +62,7 @@ def tile_routed_moe_kernel(tc, xT, w_words, w_scales, gate, offs, out):
         for g in range(2):
             nc.gpsimd.memset(xs[g][:], 0)
         for a in range(A):
-            nc.gpsimd.memset(xw[a][:, T:], 0)
+            nc.vector.memset(xw[a][:, T:], 0)
         nc.vector.memset(ws[:], 0)
 
         xv = xT.rearrange("(a p t) n -> a p t n", p=P, t=R)
@@ -122,20 +122,24 @@ def tile_routed_moe_kernel(tc, xT, w_words, w_scales, gate, offs, out):
                     )
 
         for a in range(A):
-            for lo, mid, hi in SHARE[a]:
-                cast(nc.scalar.copy, a, lo, mid)
-                cast(nc.vector.tensor_copy, a, mid, hi)
+            for engine, lo, hi in CASTS[a]:
+                cast({"S": nc.scalar.copy, "V": nc.vector.tensor_copy}[engine], a, lo, hi)
+            for lo, hi in ((0, 512), (512, 768)):
                 quantize(a, lo, hi)
-            if a < A - 1:
-                gather(gw[a], xw[a][:].bitcast(U32), 0, E * C)
-            if a == 1:
+            if a > 0:
+                gather(gw[a - 1], xw[a - 1][:].bitcast(U32), 0, E * C)
+            if a == 2:
                 gather(gs[0], xs[0][:], 0, E * C)
         for lo, hi in ((0, 384), (384, 768)):
             gather(gs[1], xs[1][:], lo, hi)
             gather(gw[A - 1], xw[A - 1][:].bitcast(U32), lo, hi)
         for b in range(len(BACK)):
             multiply(b)
-        for b, (lo, hi) in enumerate(BACK):
-            nc.vector.tensor_tensor(z[b][:], acc[b][:], gt[:, lo:hi], MULT)
-            nc.vector.tensor_copy(window[:].indirect(offsets[:, lo // 16 : hi // 16]), z[b][:])
+        for run in ((0,), (1, 2)):
+            for b in run:
+                lo, hi = BACK[b]
+                nc.vector.tensor_tensor(z[b][:], acc[b][:], gt[:, lo:hi], MULT)
+            for b in run:
+                lo, hi = BACK[b]
+                nc.vector.tensor_copy(window[:].indirect(offsets[:, lo // 16 : hi // 16]), z[b][:])
         nc.sync.dma_start(out=out, in_=window[:])

from contextlib import ExitStack

import concourse.mybir as mybir

K, T, E, C, N = 3072, 768, 6, 128, 128
FLOPS = 2 * K * N * E * C

F32 = mybir.dt.float32
BF16 = mybir.dt.bfloat16
I32 = mybir.dt.int32
U32 = mybir.dt.uint32
U16 = mybir.dt.uint16
U8 = mybir.dt.uint8
FP8X4 = mybir.dt.float8_e4m3fn_x4
MULT = mybir.AluOpType.mult

P = 128
R = 4
A = K // (P * R)
WIN = 1024
GROUP = (0, 0, 1, 1, 1, 1)
PLANE = (0, 4, 0, 4, 8, 12)
LOADS = (
    ((0, 512), (512, 768)),
    ((0, 512), (512, 768)),
    ((0, 768),),
    ((0, 768),),
    ((0, 768),),
    ((0, 512), (512, 768)),
)
CASTS = (
    (("S", 0, 192), ("V", 192, 512), ("S", 512, 640), ("V", 640, 768)),
    (("S", 0, 288), ("V", 288, 512), ("S", 512, 640), ("V", 640, 768)),
    (("S", 0, 512), ("S", 512, 576), ("V", 576, 768)),
    (("S", 0, 512), ("S", 512, 640), ("V", 640, 768)),
    (("S", 0, 512), ("S", 512, 640), ("V", 640, 768)),
    (("S", 0, 320), ("V", 320, 512), ("S", 512, 640), ("V", 640, 768)),
)
BACK = ((0, 384), (384, 640), (640, 768))


def tile_routed_moe_kernel(tc, xT, w_words, w_scales, gate, offs, out):
    nc = tc.nc
    with ExitStack() as ctx:
        keep = ctx.enter_context(tc.tile_pool(name="keep", bufs=1))
        psum = ctx.enter_context(tc.psum_pool(name="psum", bufs=1))

        offsets = keep.tile([P, E * C // 16], U16, name="offsets")
        w = keep.tile([P, E, A, N], I32, name="w", align_bytes=256)
        ws = keep.tile([P, E * A, N // 4], I32, name="ws", align_bytes=256)
        gt = keep.tile([P, E * C], F32, name="gt")
        xs = [keep.tile([P, WIN], U8, name=f"xs{g}", align_bytes=256) for g in range(2)]
        gs = [keep.tile([P, E * C], U8, name=f"gs{g}", align_bytes=256) for g in range(2)]
        raw = [keep.tile([P, R, T], F32, name=f"raw{a}", align_bytes=256) for a in range(A)]
        grp = [keep.tile([P, T, R], BF16, name=f"grp{a}", align_bytes=256) for a in range(A)]
        xw = [keep.tile([P, WIN], I32, name=f"xw{a}", align_bytes=256) for a in range(A)]
        gw = [keep.tile([P, E * C], U32, name=f"gw{a}", align_bytes=256) for a in range(A)]
        z = [keep.tile([P, hi - lo], F32, name=f"z{lo}") for lo, hi in BACK]
        window = keep.tile([P, T], F32, name="window")
        acc = [psum.tile([P, hi - lo], F32, name=f"acc{lo}") for lo, hi in BACK]

        for g in range(2):
            nc.gpsimd.memset(xs[g][:], 0)
        for a in range(A):
            nc.vector.memset(xw[a][:, T:], 0)
        nc.vector.memset(ws[:], 0)

        xv = xT.rearrange("(a p t) n -> a p t n", p=P, t=R)
        sv = w_scales.bitcast(I32).rearrange("e a q n -> q (e a) n")

        def load_x(a):
            for lo, hi in LOADS[a]:
                nc.sync.dma_start(out=raw[a][:, :, lo:hi], in_=xv[a][:, :, lo:hi])

        def load_w(e):
            nc.sync.dma_start(out=w[:, e], in_=w_words[e].rearrange("a p n r -> p a (n r)").bitcast(I32))

        def load_scales():
            for q in range(4):
                nc.sync.dma_start(out=ws[32 * q : 32 * q + 4], in_=sv[4 * q : 4 * q + 4])

        load_x(0)
        nc.sync.dma_start(offsets[:], offs)
        for a in range(1, A):
            load_x(a)
        load_scales()
        for e in range(E):
            if e == E // 2:
                nc.sync.dma_start(out=gt[:], in_=gate)
            load_w(e)

        def cast(engine_copy, a, lo, hi):
            if hi > lo:
                engine_copy(
                    out=grp[a][:, lo:hi, :].rearrange("p (c i) t -> p c t i", i=4),
                    in_=raw[a][:, :, lo:hi].rearrange("p t (c i) -> p c t i", i=4),
                )

        def quantize(a, lo, hi):
            nc.vector.quantize_mx(
                out=xw[a][:, lo:hi].bitcast(FP8X4),
                scales=xs[GROUP[a]][PLANE[a] : P, lo:hi],
                in_=grp[a][:, lo:hi, :].rearrange("p n t -> p (n t)"),
            )

        def gather(dst, source, lo, hi):
            nc.vector.tensor_copy(dst[:, lo:hi], source.indirect(offsets[:, lo // 16 : hi // 16]))

        def multiply(b):
            first, last = BACK[b]
            for e in range(first // C, last // C):
                slots = slice(e * C, (e + 1) * C)
                for a in range(A):
                    nc.tensor.matmul_mx(
                        out=acc[b][:, e * C - first : (e + 1) * C - first],
                        lhsT=w[:, e, a, :].bitcast(FP8X4),
                        lhsT_scale=ws[:, e * A + a, :].bitcast(U8),
                        rhs=gw[a][:, slots].bitcast(FP8X4),
                        rhs_scale=gs[GROUP[a]][PLANE[a] : P, slots],
                        start=(a == 0),
                        stop=(a == A - 1),
                    )

        for a in range(A):
            for engine, lo, hi in CASTS[a]:
                cast({"S": nc.scalar.copy, "V": nc.vector.tensor_copy}[engine], a, lo, hi)
            for lo, hi in ((0, 512), (512, 768)):
                quantize(a, lo, hi)
            if a > 0:
                gather(gw[a - 1], xw[a - 1][:].bitcast(U32), 0, E * C)
            if a == 2:
                gather(gs[0], xs[0][:], 0, E * C)
        for lo, hi in ((0, 384), (384, 768)):
            gather(gs[1], xs[1][:], lo, hi)
            gather(gw[A - 1], xw[A - 1][:].bitcast(U32), lo, hi)
        for b in range(len(BACK)):
            multiply(b)
        for run in ((0,), (1, 2)):
            for b in run:
                lo, hi = BACK[b]
                nc.vector.tensor_tensor(z[b][:], acc[b][:], gt[:, lo:hi], MULT)
            for b in run:
                lo, hi = BACK[b]
                nc.vector.tensor_copy(window[:].indirect(offsets[:, lo // 16 : hi // 16]), z[b][:])
        nc.sync.dma_start(out=out, in_=window[:])
